import numpy as np
import ml_dtypes


def mxq(x, axis, fmt="e4m3"):
    dtype, down = {"e4m3": (ml_dtypes.float8_e4m3fn, 7), "e5m2": (ml_dtypes.float8_e5m2, 14)}[fmt]
    v = np.moveaxis(np.asarray(x, np.float32).astype(ml_dtypes.bfloat16).astype(np.float64), axis, -1)
    blocks = v.reshape(v.shape[:-1] + (-1, 32))
    amax = np.abs(blocks).max(-1, keepdims=True)
    byte = np.maximum(np.where(amax > 0, np.frexp(amax)[1] - 1 + 127, 0) - down, 1)
    scale = np.exp2(byte - 127.0)
    codes = (blocks / scale).astype(np.float32).astype(dtype).astype(np.float64)
    return np.moveaxis((codes * scale).reshape(v.shape), -1, axis)


WIDE = False


def mx_kscale(k):
    if not WIDE:
        return np.ones(k)
    levels = np.array([10, -10, 5, -5, 0])
    if k % 512:
        return np.exp2(np.random.permutation(np.resize(levels, k // 32))).repeat(32)
    a = np.empty((k // 512, 16))
    for p in range(k // 512):
        a[p, :8] = np.random.permutation(np.resize(levels, 8))
        for g in range(8):
            far = levels[np.abs(levels - a[p, g]) >= 10]
            a[p, g + 8] = far[np.random.randint(len(far))]
    return np.exp2(a.ravel()).repeat(32)


def f64(x):
    return np.asarray(x).astype(np.float64)


def striped(idx):
    return np.tile(idx.reshape(-1, 16).T, (8, 1)).astype(np.uint16)


def unstriped(offs):
    return offs[:16].T.reshape(-1).astype(np.int64)


def pack_weight(w):
    k, n = w.shape
    w = f64(np.asarray(w, np.float32).astype(ml_dtypes.bfloat16)).reshape(k // 32, 32, n)
    amax = np.abs(w).max(1)
    byte = np.clip(np.where(amax > 0, np.frexp(amax)[1] - 1 + 127 - 7, 1), 1, 254)
    scaled = (w * np.exp2(127.0 - byte)[:, None, :]).reshape(k, n).astype(np.float32)
    words = np.ascontiguousarray(scaled.reshape(k // 512, 128, 4, n).transpose(0, 1, 3, 2)).astype(ml_dtypes.float8_e4m3fn).view(np.uint8)
    return words, np.ascontiguousarray(byte.astype(np.uint8).reshape(k // 512, 16, n))


def unpack_weight(words, scales):
    g, p, n, _ = words.shape
    vals = np.ascontiguousarray(words).view(ml_dtypes.float8_e4m3fn).astype(np.float64) * np.repeat(np.exp2(scales.astype(np.float64) - 127.0), 8, axis=1)[..., None]
    return vals.transpose(0, 1, 3, 2).reshape(g * 512, n)


K, T, S, N, W = 512, 2048, 512, 512, 2048
P = 2 ** 7


def setup_inputs():
    n = np.random.standard_normal
    s = mx_kscale(K)[:, None]
    c = mx_kscale(S)
    packed_xT = pack_weight(n((K, T)) * s)
    packed_eT = pack_weight(n((K, W)) * s)
    return {
        "x_words": packed_xT[0],
        "x_scales": packed_xT[1],
        "e_words": packed_eT[0],
        "e_scales": packed_eT[1],
        "wa": (n((K, N)) / np.sqrt(K) / s).astype(np.float32),
        "mean": (np.tile(0.2 * n(N), (P, 1))).astype(np.float32),
        "wgt": (np.random.uniform(0.5, 1.0, (S, 1)) * c[:, None] / np.sqrt(S)).astype(np.float32),
        "wb": (n((K, N)) / np.sqrt(K) / s).astype(np.float32),
        "inv": (np.random.uniform(0.6, 1.4, (S, 1)) / c[:, None]).astype(np.float32),
        "goal": (np.eye(N) * np.random.uniform(0.8, 1.2, N)).astype(np.float32),
        "lam": (np.random.uniform(0.1, 1.0, (N, N))).astype(np.float32),
        "offs": striped(np.random.permutation(T)[:S]),
        "par": striped(np.random.permutation(W)[:S]),
    }


def reference(x_words, x_scales, e_words, e_scales, wa, mean, wgt, wb, inv, goal, lam, offs, par):
    xq = unpack_weight(x_words, x_scales)[:, unstriped(offs)]
    waq = mxq(f64(wa), 0, "e4m3")
    a = f64(wgt) * ((xq.T @ waq) - f64(mean)[:1])
    e_par = unpack_weight(e_words, e_scales)[:, unstriped(par)]
    wbq = mxq(f64(wb), 0, "e4m3")
    vv = f64(inv) * (e_par.T @ wbq)
    z = mxq(a, 0, "e4m3").T @ mxq(vv, 0, "e4m3")
    dd = z - f64(goal)
    return (dd * f64(lam)) * dd

@@ -1,0 +1,211 @@
+from contextlib import ExitStack
+
+import concourse.mybir as mybir
+
+K, T, S, N = 512, 2048, 512, 512
+FLOPS = 3 * 2 * 512 * 512 * 512
+
+F32 = mybir.dt.float32
+BF16 = mybir.dt.bfloat16
+I32 = mybir.dt.int32
+U32 = mybir.dt.uint32
+U16 = mybir.dt.uint16
+U8 = mybir.dt.uint8
+FP8X4 = mybir.dt.float8_e4m3fn_x4
+ALU = mybir.AluOpType
+ACT = mybir.ActivationFunctionType
+
+P = 128
+PACK = 4
+CHUNKS = N // P
+HALF = N // 2
+
+
+def tile_picked_ybarlow_loss_p_kernel(
+    tc, x_words, x_scales, e_words, e_scales, wa, mean, wgt, wb, inv, goal, lam, offs, par, out
+):
+    nc = tc.nc
+    with ExitStack() as ctx:
+        keep = ctx.enter_context(tc.tile_pool(name="keep", bufs=1))
+        acc_pool = ctx.enter_context(tc.psum_pool(name="acc", bufs=4))
+        turn_pool = ctx.enter_context(tc.psum_pool(name="turn", bufs=2))
+        z_pool = ctx.enter_context(tc.psum_pool(name="z", bufs=2))
+
+        def sb(shape, dtype, name, tag=None):
+            return keep.tile(shape, dtype, name=name, tag=tag or name, align_bytes=64)
+
+        par_sb = keep.tile([P, S // 16], U16, name="par_sb")
+        offs_sb = keep.tile([P, S // 16], U16, name="offs_sb")
+        e_bytes = sb([P, T], U8, "e_bytes")
+        x_bytes = sb([P, T], U8, "x_bytes")
+        e_table = sb([P, T], U32, "e_table")
+        nc.vector.memset(e_bytes[:].bitcast(I32), 0)
+        warm = sb([P, 2], F32, "warm")
+        nc.vector.memset(warm[:, 0:1], 0.0)
+        zeros = sb([P, P], F32, "zeros", tag="stream0")
+        nc.vector.memset(zeros[:], 0.0)
+        nc.vector.memset(x_bytes[:].bitcast(I32), 0)
+        mean_rows = sb([P, P], F32, "mean_rows")
+        nc.vector.memset(mean_rows[:], 0.0)
+
+        def load_scales(tile, scales, row0):
+            for q in range(4):
+                nc.scalar.dma_start(
+                    out=tile[32 * q + row0 : 32 * q + row0 + 4, :].bitcast(I32),
+                    in_=scales[0, 4 * q : 4 * q + 4, :].bitcast(I32),
+                )
+
+        def load_words(tile, words):
+            nc.sync.dma_start(out=tile[:].bitcast(I32), in_=words[0].rearrange("p n t -> p (n t)").bitcast(I32))
+
+        def load_weight(w, name):
+            halves = []
+            for h in range(2):
+                raw = sb([P, PACK, HALF], F32, "%s_raw%d" % (name, h), tag="stream%d" % h)
+                nc.sync.dma_start(out=raw[:], in_=w.rearrange("(p j) c -> p j c", j=PACK)[:, :, h * HALF : (h + 1) * HALF])
+                halves.append(raw)
+            return halves
+
+        E_ROW, X_ROW = 0, 4
+        nc.sync.dma_start(par_sb[:], par)
+        nc.sync.dma_start(offs_sb[:], offs)
+        load_words(e_table, e_words)
+        inv_col = sb([P, PACK], F32, "inv_col", tag="stream1")
+        wgt_col = sb([P, PACK], F32, "wgt_col", tag="x_slot")
+        nc.scalar.dma_start(out=inv_col[:], in_=inv.rearrange("(p j) o -> p (j o)", j=PACK))
+        nc.scalar.dma_start(out=wgt_col[:], in_=wgt.rearrange("(p j) o -> p (j o)", j=PACK))
+        load_scales(e_bytes, e_scales, E_ROW)
+        nc.scalar.activation(out=warm[:, 1:2], in_=warm[:, 0:1], func=ACT.Square)
+        load_scales(x_bytes, x_scales, X_ROW)
+
+        ident = sb([P, P], F32, "ident")
+        nc.gpsimd.affine_select(
+            out=ident[:], in_=zeros[:], compare_op=ALU.not_equal, fill=1.0, base=0, pattern=[[-1, P]], channel_multiplier=1
+        )
+        nc.gpsimd.dma_start(out=mean_rows[0:CHUNKS, :], in_=mean[0:1, :].rearrange("o (c q) -> (o c) q", q=P))
+        goal_col = sb([P, CHUNKS], F32, "goal_col")
+        with nc.allow_non_contiguous_dma(reason="the diagonal of goal"):
+            nc.gpsimd.dma_start(
+                out=goal_col[:],
+                in_=goal.rearrange("a b -> (a b)")[0 : N * N : N + 1].rearrange("(c q) -> q c", q=P),
+            )
+
+        def spread(col, name):
+            bank = acc_pool.tile([P, PACK, P], F32, name="acc", tag="acc")
+            for j in range(PACK):
+                nc.tensor.transpose(bank[:, j, :], col[:, j : j + 1].to_broadcast([P, P]), ident[:])
+            row = sb([P, P, PACK], F32, name)
+            nc.scalar.activation(out=row[:], in_=bank[:].rearrange("q j p -> q p j"), func=ACT.Copy)
+            return row[:].rearrange("q p j -> q (p j)")
+
+        inv_row = spread(inv_col, "inv_row")
+        wgt_row = spread(wgt_col, "wgt_row")
+        mean_bank = turn_pool.tile([P, 2, P], F32, name="turned", tag="turned")
+        nc.tensor.transpose(mean_bank[:, 0, :], mean_rows[:], ident[:])
+        mean_col = sb([P, CHUNKS], F32, "mean_col")
+        nc.scalar.copy(out=mean_col[:], in_=mean_bank[:, 0, 0:CHUNKS])
+
+        wb_raw = load_weight(wb, "wb")
+        x_table = sb([P, T], U32, "x_table", tag="x_slot")
+        load_words(x_table, x_words)
+
+        def gather(window, dtype, offsets, name, tag=None):
+            picked = sb([P, S], dtype, name, tag)
+            nc.vector.tensor_copy(picked[:], window[:].indirect(offsets[:]))
+            return picked
+
+        def quantize(grouped, codes, scales):
+            nc.vector.quantize_mx(out=codes.bitcast(FP8X4), scales=scales, in_=grouped[:].rearrange("p c j -> p (c j)"))
+
+        def weight_chunk(halves, c, name):
+            raw = halves[c // 2][:, :, (c % 2) * P : (c % 2 + 1) * P]
+            grouped = sb([P, P, PACK], BF16, "%s_grouped%d" % (name, c))
+            nc.scalar.copy(
+                out=grouped[:].rearrange("p (c i) j -> p c j i", i=4),
+                in_=raw.rearrange("p j (c i) -> p c j i", i=4),
+            )
+            codes = sb([P, P], U32, "%s_codes%d" % (name, c))
+            scales = sb([P, P], U8, "%s_scales%d" % (name, c))
+            quantize(grouped, codes[:], scales[:])
+            return codes, scales
+
+        def project(w_chunk, picked, row0):
+            bank = acc_pool.tile([P, S], F32, name="acc", tag="acc")
+            nc.tensor.matmul_mx(
+                out=bank[:],
+                lhsT=w_chunk[0][:].bitcast(FP8X4),
+                lhsT_scale=w_chunk[1][:],
+                rhs=picked[0][:].bitcast(FP8X4),
+                rhs_scale=picked[1][row0:P, :],
+                start=True,
+                stop=True,
+            )
+            return bank
+
+        def turn(rounded, name):
+            words = rounded[:].bitcast(F32)
+            bank = turn_pool.tile([P, 2, P], F32, name="turned", tag="turned")
+            for u in range(2):
+                nc.tensor.transpose(bank[:, u, :], words[:, u : S // 2 : 2], ident[:])
+            grouped = sb([P, P, PACK], BF16, name)
+            nc.scalar.copy(out=grouped[:].bitcast(F32), in_=bank[:].rearrange("p u r -> p r u"))
+            return grouped
+
+        e_scales_picked = gather(e_bytes, U8, par_sb, "e_scales_picked")
+        e_picked = (gather(e_table, U32, par_sb, "e_codes_picked", tag="e_bytes"), e_scales_picked)
+
+        v_codes = sb([P, N], U32, "v_codes")
+        v_scales = sb([P, N], U8, "v_scales")
+        wb_q = [weight_chunk(wb_raw, c, "wb") for c in range(CHUNKS)]
+        x_scales_picked = gather(x_bytes, U8, offs_sb, "x_scales_picked", tag="wb_grouped0")
+        v_banks = [project(wb_q[c], e_picked, E_ROW) for c in range(CHUNKS)]
+        v_grouped = []
+        for c in range(CHUNKS):
+            rounded = sb([P, S], BF16, "v_rounded%d" % c)
+            nc.vector.tensor_tensor(rounded[:], v_banks[c][:], inv_row, ALU.mult)
+            v_grouped.append(turn(rounded, "v_grouped%d" % c))
+
+        x_picked = (gather(x_table, U32, offs_sb, "x_codes_picked"), x_scales_picked)
+        for c in range(CHUNKS):
+            cols = slice(c * P, (c + 1) * P)
+            quantize(v_grouped[c], v_codes[:, cols], v_scales[:, cols])
+
+        wa_raw = load_weight(wa, "wa")
+        wa_q = [weight_chunk(wa_raw, c, "wa") for c in range(CHUNKS)]
+        lam_sb = []
+        for h in range(2):
+            pair = sb([P, 2, N], F32, "lam%d" % h, tag=("wb_grouped3", "wb_codes3")[h])
+            nc.sync.dma_start(out=pair[:], in_=lam[h * HALF : (h + 1) * HALF, :].rearrange("(c p) n -> p c n", p=P))
+            lam_sb.extend([pair[:, 0, :], pair[:, 1, :]])
+        a_grouped = []
+        for c in range(CHUNKS):
+            bank = project(wa_q[c], x_picked, X_ROW)
+            rounded = sb([P, S], BF16, "a_rounded%d" % c)
+            nc.vector.scalar_tensor_tensor(rounded[:], bank[:], mean_col[:, c : c + 1], wgt_row, ALU.subtract, ALU.mult)
+            a_grouped.append(turn(rounded, "a_grouped%d" % c))
+
+        for c in range(CHUNKS):
+            cols = slice(c * P, (c + 1) * P)
+            a_codes = sb([P, P], U32, "a_codes%d" % c)
+            a_scales = sb([P, P], U8, "a_scales%d" % c)
+            quantize(a_grouped[c], a_codes[:], a_scales[:])
+            z = z_pool.tile([P, N], F32, name="z", tag="z")
+            nc.tensor.matmul_mx(
+                out=z[:],
+                lhsT=a_codes[:].bitcast(FP8X4),
+                lhsT_scale=a_scales[:],
+                rhs=v_codes[:].bitcast(FP8X4),
+                rhs_scale=v_scales[:],
+                start=True,
+                stop=True,
+            )
+            missed = sb([P, P], F32, "missed%d" % c)
+            nc.vector.scalar_tensor_tensor(missed[:], ident[:], goal_col[:, c : c + 1], z[:, cols], ALU.mult, ALU.subtract)
+            squared = sb([P, N], F32, "squared%d" % c)
+            for lo, hi in ((0, c * P), ((c + 1) * P, N)):
+                if hi > lo:
+                    nc.scalar.activation(out=squared[:, lo:hi], in_=z[:, lo:hi], func=ACT.Square)
+            nc.scalar.activation(out=squared[:, cols], in_=missed[:], func=ACT.Square)
+            result = sb([P, N], F32, "result%d" % c)
+            nc.vector.tensor_tensor(result[:], squared[:], lam_sb[c], ALU.mult)
+            nc.sync.dma_start(out=out[cols, :], in_=result[:])

@@ -1,6 +1,7 @@
 from contextlib import ExitStack
 
 import concourse.mybir as mybir
+from concourse.masks import make_identity
 
 K, T, S, N = 512, 2048, 512, 512
 FLOPS = 3 * 2 * 512 * 512 * 512
@@ -29,7 +30,7 @@ def tile_picked_ybarlow_loss_p_kernel(
         keep = ctx.enter_context(tc.tile_pool(name="keep", bufs=1))
         acc_pool = ctx.enter_context(tc.psum_pool(name="acc", bufs=4))
         turn_pool = ctx.enter_context(tc.psum_pool(name="turn", bufs=2))
-        z_pool = ctx.enter_context(tc.psum_pool(name="z", bufs=2))
+        spread_pool = ctx.enter_context(tc.psum_pool(name="spread", bufs=2))
 
         def sb(shape, dtype, name, tag=None):
             return keep.tile(shape, dtype, name=name, tag=tag or name, align_bytes=64)
@@ -38,19 +39,15 @@ def tile_picked_ybarlow_loss_p_kernel(
         offs_sb = keep.tile([P, S // 16], U16, name="offs_sb")
         e_bytes = sb([P, T], U8, "e_bytes")
         x_bytes = sb([P, T], U8, "x_bytes")
-        e_table = sb([P, T], U32, "e_table")
-        nc.vector.memset(e_bytes[:].bitcast(I32), 0)
-        warm = sb([P, 2], F32, "warm")
-        nc.vector.memset(warm[:, 0:1], 0.0)
-        zeros = sb([P, P], F32, "zeros", tag="stream0")
-        nc.vector.memset(zeros[:], 0.0)
+        ident = sb([P, P], F32, "ident")
+        nc.gpsimd.memset(ident[:], 0.0)
+        nc.gpsimd.memset(e_bytes[:].bitcast(I32), 0)
+        make_identity(nc, ident[:], nomemset=True)
         nc.vector.memset(x_bytes[:].bitcast(I32), 0)
-        mean_rows = sb([P, P], F32, "mean_rows")
-        nc.vector.memset(mean_rows[:], 0.0)
 
-        def load_scales(tile, scales, row0):
+        def load_scales(queue, tile, scales, row0):
             for q in range(4):
-                nc.scalar.dma_start(
+                queue.dma_start(
                     out=tile[32 * q + row0 : 32 * q + row0 + 4, :].bitcast(I32),
                     in_=scales[0, 4 * q : 4 * q + 4, :].bitcast(I32),
                 )
@@ -58,56 +55,51 @@ def tile_picked_ybarlow_loss_p_kernel(
         def load_words(tile, words):
             nc.sync.dma_start(out=tile[:].bitcast(I32), in_=words[0].rearrange("p n t -> p (n t)").bitcast(I32))
 
-        def load_weight(w, name):
-            halves = []
-            for h in range(2):
-                raw = sb([P, PACK, HALF], F32, "%s_raw%d" % (name, h), tag="stream%d" % h)
-                nc.sync.dma_start(out=raw[:], in_=w.rearrange("(p j) c -> p j c", j=PACK)[:, :, h * HALF : (h + 1) * HALF])
-                halves.append(raw)
-            return halves
+        def load_half(w, h, name, tag):
+            raw = sb([P, PACK, HALF], F32, name, tag)
+            nc.sync.dma_start(out=raw[:], in_=w.rearrange("(p j) c -> p j c", j=PACK)[:, :, h * HALF : (h + 1) * HALF])
+            return raw
 
         E_ROW, X_ROW = 0, 4
         nc.sync.dma_start(par_sb[:], par)
-        nc.sync.dma_start(offs_sb[:], offs)
+        inv_col = sb([P, PACK], F32, "inv_col")
+        nc.sync.dma_start(out=inv_col[:], in_=inv.rearrange("(p j) o -> p (j o)", j=PACK))
+        wb_raw = [load_half(wb, 0, "wb_raw0", "wb_raw0")]
+        load_scales(nc.sync, e_bytes, e_scales, E_ROW)
+        e_table = sb([P, T], U32, "e_table", tag="e_slot")
         load_words(e_table, e_words)
-        inv_col = sb([P, PACK], F32, "inv_col", tag="stream1")
-        wgt_col = sb([P, PACK], F32, "wgt_col", tag="x_slot")
-        nc.scalar.dma_start(out=inv_col[:], in_=inv.rearrange("(p j) o -> p (j o)", j=PACK))
-        nc.scalar.dma_start(out=wgt_col[:], in_=wgt.rearrange("(p j) o -> p (j o)", j=PACK))
-        load_scales(e_bytes, e_scales, E_ROW)
-        nc.scalar.activation(out=warm[:, 1:2], in_=warm[:, 0:1], func=ACT.Square)
-        load_scales(x_bytes, x_scales, X_ROW)
-
-        ident = sb([P, P], F32, "ident")
-        nc.gpsimd.affine_select(
-            out=ident[:], in_=zeros[:], compare_op=ALU.not_equal, fill=1.0, base=0, pattern=[[-1, P]], channel_multiplier=1
-        )
-        nc.gpsimd.dma_start(out=mean_rows[0:CHUNKS, :], in_=mean[0:1, :].rearrange("o (c q) -> (o c) q", q=P))
+        nc.sync.dma_start(offs_sb[:], offs)
+        load_scales(nc.sync, x_bytes, x_scales, X_ROW)
+        wb_raw.append(load_half(wb, 1, "wb_raw1", "wb_raw1"))
+        x_table = sb([P, T], U32, "x_table")
+        load_words(x_table, x_words)
+        wa_raw = [load_half(wa, h, "wa_raw%d" % h, None) for h in range(2)]
+        mean_col = sb([P, CHUNKS], F32, "mean_col")
         goal_col = sb([P, CHUNKS], F32, "goal_col")
-        with nc.allow_non_contiguous_dma(reason="the diagonal of goal"):
-            nc.gpsimd.dma_start(
+        with nc.allow_non_contiguous_dma(reason="one value a partition"):
+            nc.sync.dma_start(out=mean_col[:], in_=mean[0, :].rearrange("(c q) -> q c", q=P))
+            nc.sync.dma_start(
                 out=goal_col[:],
                 in_=goal.rearrange("a b -> (a b)")[0 : N * N : N + 1].rearrange("(c q) -> q c", q=P),
             )
+        lam_sb = []
+        for h in range(2):
+            pair = sb([P, 2, N], F32, "lam%d" % h)
+            nc.sync.dma_start(out=pair[:], in_=lam[h * HALF : (h + 1) * HALF, :].rearrange("(c p) n -> p c n", p=P))
+            lam_sb.extend([pair[:, 0, :], pair[:, 1, :]])
 
-        def spread(col, name):
-            bank = acc_pool.tile([P, PACK, P], F32, name="acc", tag="acc")
+        wgt_col = sb([P, PACK], F32, "wgt_col")
+        nc.gpsimd.dma_start(out=wgt_col[:], in_=wgt.rearrange("(p j) o -> p (j o)", j=PACK))
+
+        def spread(col, name, tag=None):
+            bank = spread_pool.tile([P, PACK, P], F32, name="spread", tag="spread")
             for j in range(PACK):
                 nc.tensor.transpose(bank[:, j, :], col[:, j : j + 1].to_broadcast([P, P]), ident[:])
-            row = sb([P, P, PACK], F32, name)
+            row = sb([P, P, PACK], F32, name, tag)
             nc.scalar.activation(out=row[:], in_=bank[:].rearrange("q j p -> q p j"), func=ACT.Copy)
             return row[:].rearrange("q p j -> q (p j)")
 
         inv_row = spread(inv_col, "inv_row")
-        wgt_row = spread(wgt_col, "wgt_row")
-        mean_bank = turn_pool.tile([P, 2, P], F32, name="turned", tag="turned")
-        nc.tensor.transpose(mean_bank[:, 0, :], mean_rows[:], ident[:])
-        mean_col = sb([P, CHUNKS], F32, "mean_col")
-        nc.scalar.copy(out=mean_col[:], in_=mean_bank[:, 0, 0:CHUNKS])
-
-        wb_raw = load_weight(wb, "wb")
-        x_table = sb([P, T], U32, "x_table", tag="x_slot")
-        load_words(x_table, x_words)
 
         def gather(window, dtype, offsets, name, tag=None):
             picked = sb([P, S], dtype, name, tag)
@@ -142,58 +134,82 @@ def tile_picked_ybarlow_loss_p_kernel(
             )
             return bank
 
-        def turn(rounded, name):
-            words = rounded[:].bitcast(F32)
-            bank = turn_pool.tile([P, 2, P], F32, name="turned", tag="turned")
-            for u in range(2):
-                nc.tensor.transpose(bank[:, u, :], words[:, u : S // 2 : 2], ident[:])
-            grouped = sb([P, P, PACK], BF16, name)
-            nc.scalar.copy(out=grouped[:].bitcast(F32), in_=bank[:].rearrange("p u r -> p r u"))
+        def turn(chunks, name, tag=None):
+            bank = turn_pool.tile([P, len(chunks), 2, P], F32, name="turned", tag="turned")
+            for c, rounded in enumerate(chunks):
+                words = rounded[:].bitcast(F32)
+                for u in range(2):
+                    nc.tensor.transpose(bank[:, c, u, :], words[:, u : S // 2 : 2], ident[:])
+            grouped = sb([P, len(chunks) * P, PACK], BF16, name, tag)
+            nc.scalar.copy(
+                out=grouped[:].bitcast(F32).rearrange("p (c r) u -> p c r u", r=P),
+                in_=bank[:].rearrange("p c u r -> p c r u"),
+            )
             return grouped
 
         e_scales_picked = gather(e_bytes, U8, par_sb, "e_scales_picked")
-        e_picked = (gather(e_table, U32, par_sb, "e_codes_picked", tag="e_bytes"), e_scales_picked)
+        e_picked = (gather(e_table, U32, par_sb, "e_codes_picked"), e_scales_picked)
 
         v_codes = sb([P, N], U32, "v_codes")
         v_scales = sb([P, N], U8, "v_scales")
-        wb_q = [weight_chunk(wb_raw, c, "wb") for c in range(CHUNKS)]
-        x_scales_picked = gather(x_bytes, U8, offs_sb, "x_scales_picked", tag="wb_grouped0")
+        first = sb([P, HALF, PACK], BF16, "wb_first")
+        nc.scalar.copy(
+            out=first[:].rearrange("p (c i) j -> p c j i", i=4), in_=wb_raw[0][:].rearrange("p j (c i) -> p c j i", i=4)
+        )
+        first_codes = sb([P, HALF], U32, "wb_first_codes", "e_bytes")
+        first_scales = sb([P, HALF], U8, "wb_first_scales")
+        quantize(first, first_codes[:], first_scales[:])
+        wb_q = [(first_codes[:, c * P : (c + 1) * P], first_scales[:, c * P : (c + 1) * P]) for c in range(2)]
+        wb_q.extend(weight_chunk(wb_raw, c, "wb") for c in range(2, CHUNKS))
+        x_scales_picked = gather(x_bytes, U8, offs_sb, "x_scales_picked")
+        v_rounded = {}
         v_banks = [project(wb_q[c], e_picked, E_ROW) for c in range(CHUNKS)]
-        v_grouped = []
-        for c in range(CHUNKS):
-            rounded = sb([P, S], BF16, "v_rounded%d" % c)
+
+        v_first = sb([P, 2, S], BF16, "v_first", "wb_raw1")
+
+        def e_step(c):
+            rounded = v_first[:, c, :] if c < 2 else sb([P, S], BF16, "v_rounded%d" % c, {"2":"wa_grouped0","3":"wa_raw0"}.get(str(c)))
             nc.vector.tensor_tensor(rounded[:], v_banks[c][:], inv_row, ALU.mult)
-            v_grouped.append(turn(rounded, "v_grouped%d" % c))
+            v_rounded[c] = rounded
 
         x_picked = (gather(x_table, U32, offs_sb, "x_codes_picked"), x_scales_picked)
-        for c in range(CHUNKS):
-            cols = slice(c * P, (c + 1) * P)
-            quantize(v_grouped[c], v_codes[:, cols], v_scales[:, cols])
+        e_step(0)
+        e_step(1)
 
-        wa_raw = load_weight(wa, "wa")
-        wa_q = [weight_chunk(wa_raw, c, "wa") for c in range(CHUNKS)]
-        lam_sb = []
-        for h in range(2):
-            pair = sb([P, 2, N], F32, "lam%d" % h, tag=("wb_grouped3", "wb_codes3")[h])
-            nc.sync.dma_start(out=pair[:], in_=lam[h * HALF : (h + 1) * HALF, :].rearrange("(c p) n -> p c n", p=P))
-            lam_sb.extend([pair[:, 0, :], pair[:, 1, :]])
-        a_grouped = []
-        for c in range(CHUNKS):
+        wgt_row = spread(wgt_col, "wgt_row", "wb_grouped3")
+
+        wa_q = {}
+        a_rounded = {}
+        a_q = {}
+        zs = {}
+        sq = {}
+
+        def w_step(c):
+            wa_q[c] = weight_chunk(wa_raw, c, "wa")
+
+        def a_step(c):
             bank = project(wa_q[c], x_picked, X_ROW)
             rounded = sb([P, S], BF16, "a_rounded%d" % c)
             nc.vector.scalar_tensor_tensor(rounded[:], bank[:], mean_col[:, c : c + 1], wgt_row, ALU.subtract, ALU.mult)
-            a_grouped.append(turn(rounded, "a_grouped%d" % c))
+            a_rounded[c] = rounded
 
-        for c in range(CHUNKS):
-            cols = slice(c * P, (c + 1) * P)
+        def v_step(c):
+            cols = slice(c * HALF, (c + 1) * HALF)
+            quantize(turn([v_rounded[2 * c], v_rounded[2 * c + 1]], "v_grouped%d" % c, {"0":"wa_grouped1"}.get(str(c))), v_codes[:, cols], v_scales[:, cols])
+
+        def t_step(c):
             a_codes = sb([P, P], U32, "a_codes%d" % c)
             a_scales = sb([P, P], U8, "a_scales%d" % c)
-            quantize(a_grouped[c], a_codes[:], a_scales[:])
-            z = z_pool.tile([P, N], F32, name="z", tag="z")
+            quantize(turn([a_rounded[c]], "a_grouped%d" % c), a_codes[:], a_scales[:])
+            a_q[c] = (a_codes, a_scales)
+
+        def z_step(c):
+            cols = slice(c * P, (c + 1) * P)
+            z = acc_pool.tile([P, N], F32, name="acc", tag="acc")
             nc.tensor.matmul_mx(
                 out=z[:],
-                lhsT=a_codes[:].bitcast(FP8X4),
-                lhsT_scale=a_scales[:],
+                lhsT=a_q[c][0][:].bitcast(FP8X4),
+                lhsT_scale=a_q[c][1][:],
                 rhs=v_codes[:].bitcast(FP8X4),
                 rhs_scale=v_scales[:],
                 start=True,
@@ -206,6 +222,35 @@ def tile_picked_ybarlow_loss_p_kernel(
                 if hi > lo:
                     nc.scalar.activation(out=squared[:, lo:hi], in_=z[:, lo:hi], func=ACT.Square)
             nc.scalar.activation(out=squared[:, cols], in_=missed[:], func=ACT.Square)
+            sq[c] = squared
+
+        def o_step(c):
+            cols = slice(c * P, (c + 1) * P)
             result = sb([P, N], F32, "result%d" % c)
-            nc.vector.tensor_tensor(result[:], squared[:], lam_sb[c], ALU.mult)
+            nc.vector.tensor_tensor(result[:], sq[c][:], lam_sb[c], ALU.mult)
             nc.sync.dma_start(out=out[cols, :], in_=result[:])
+
+        w_step(0)
+        w_step(1)
+        e_step(2)
+        e_step(3)
+        w_step(2)
+        w_step(3)
+        v_step(0)
+        v_step(1)
+        a_step(0)
+        t_step(0)
+        a_step(1)
+        t_step(1)
+        a_step(2)
+        t_step(2)
+        a_step(3)
+        t_step(3)
+        z_step(0)
+        z_step(1)
+        z_step(2)
+        z_step(3)
+        o_step(0)
+        o_step(1)
+        o_step(2)
+        o_step(3)

@@ -4,7 +4,7 @@ import concourse.mybir as mybir
 from concourse.masks import make_identity
 
 K, T, S, N = 512, 2048, 512, 512
-FLOPS = 3 * 2 * 512 * 512 * 512
+FLOPS = 3 * 2 * K * S * N
 
 F32 = mybir.dt.float32
 BF16 = mybir.dt.bfloat16
@@ -20,6 +20,7 @@ P = 128
 PACK = 4
 CHUNKS = N // P
 HALF = N // 2
+E_ROW, X_ROW = 0, 4
 
 
 def tile_picked_ybarlow_loss_p_kernel(
@@ -32,225 +33,196 @@ def tile_picked_ybarlow_loss_p_kernel(
         turn_pool = ctx.enter_context(tc.psum_pool(name="turn", bufs=2))
         spread_pool = ctx.enter_context(tc.psum_pool(name="spread", bufs=2))
 
-        def sb(shape, dtype, name, tag=None):
-            return keep.tile(shape, dtype, name=name, tag=tag or name, align_bytes=64)
+        def sb(shape, dtype, name, after=None):
+            return keep.tile(shape, dtype, name=name, tag=after or name, align_bytes=64)
 
         par_sb = keep.tile([P, S // 16], U16, name="par_sb")
         offs_sb = keep.tile([P, S // 16], U16, name="offs_sb")
         e_bytes = sb([P, T], U8, "e_bytes")
         x_bytes = sb([P, T], U8, "x_bytes")
         ident = sb([P, P], F32, "ident")
+        mean_rows = sb([P, P], F32, "mean_rows")
         nc.gpsimd.memset(ident[:], 0.0)
         nc.gpsimd.memset(e_bytes[:].bitcast(I32), 0)
         make_identity(nc, ident[:], nomemset=True)
         nc.vector.memset(x_bytes[:].bitcast(I32), 0)
+        nc.vector.memset(mean_rows[:], 0.0)
 
         def load_scales(queue, tile, scales, row0):
-            for q in range(4):
-                queue.dma_start(
-                    out=tile[32 * q + row0 : 32 * q + row0 + 4, :].bitcast(I32),
-                    in_=scales[0, 4 * q : 4 * q + 4, :].bitcast(I32),
-                )
+            for r in range(4):
+                queue.dma_start(out=tile[row0 + r : P : 32, :].bitcast(I32), in_=scales[0, r:16:4, :].bitcast(I32))
 
-        def load_words(tile, words):
-            nc.sync.dma_start(out=tile[:].bitcast(I32), in_=words[0].rearrange("p n t -> p (n t)").bitcast(I32))
+        def load_words(words, name):
+            table = sb([P, T], U32, name)
+            nc.sync.dma_start(out=table[:].bitcast(I32), in_=words[0].rearrange("p n t -> p (n t)").bitcast(I32))
+            return table
 
-        def load_half(w, h, name, tag):
-            raw = sb([P, PACK, HALF], F32, name, tag)
-            nc.sync.dma_start(out=raw[:], in_=w.rearrange("(p j) c -> p j c", j=PACK)[:, :, h * HALF : (h + 1) * HALF])
-            return raw
+        def load_columns(w, lo, hi, name):
+            raw = sb([P, PACK, hi - lo], F32, name)
+            nc.sync.dma_start(out=raw[:], in_=w.rearrange("(p j) c -> p j c", j=PACK)[:, :, lo:hi])
+            return [raw[:, :, c : c + P] for c in range(0, hi - lo, P)]
 
-        E_ROW, X_ROW = 0, 4
+        def load_factor(queue, factor, name):
+            col = sb([P, PACK], F32, name)
+            queue.dma_start(out=col[:], in_=factor.rearrange("(p j) o -> p (j o)", j=PACK))
+            return col
+
         nc.sync.dma_start(par_sb[:], par)
-        inv_col = sb([P, PACK], F32, "inv_col")
-        nc.sync.dma_start(out=inv_col[:], in_=inv.rearrange("(p j) o -> p (j o)", j=PACK))
-        wb_raw = [load_half(wb, 0, "wb_raw0", "wb_raw0")]
+        inv_col = load_factor(nc.scalar, inv, "inv_col")
+        wb_raw = load_columns(wb, 0, HALF, "wb_raw01")
         load_scales(nc.sync, e_bytes, e_scales, E_ROW)
-        e_table = sb([P, T], U32, "e_table", tag="e_slot")
-        load_words(e_table, e_words)
+        e_table = load_words(e_words, "e_table")
         nc.sync.dma_start(offs_sb[:], offs)
-        load_scales(nc.sync, x_bytes, x_scales, X_ROW)
-        wb_raw.append(load_half(wb, 1, "wb_raw1", "wb_raw1"))
-        x_table = sb([P, T], U32, "x_table")
-        load_words(x_table, x_words)
-        wa_raw = [load_half(wa, h, "wa_raw%d" % h, None) for h in range(2)]
-        mean_col = sb([P, CHUNKS], F32, "mean_col")
-        goal_col = sb([P, CHUNKS], F32, "goal_col")
-        with nc.allow_non_contiguous_dma(reason="one value a partition"):
-            nc.sync.dma_start(out=mean_col[:], in_=mean[0, :].rearrange("(c q) -> q c", q=P))
-            nc.sync.dma_start(
-                out=goal_col[:],
-                in_=goal.rearrange("a b -> (a b)")[0 : N * N : N + 1].rearrange("(c q) -> q c", q=P),
-            )
+        wb_raw = wb_raw + load_columns(wb, HALF, N, "wb_raw23")
+        x_table = load_words(x_words, "x_table")
+        wa_raw = load_columns(wa, 0, HALF, "wa_raw01")
+        wa_raw = wa_raw + load_columns(wa, 2 * P, 3 * P, "wa_raw2") + load_columns(wa, 3 * P, N, "wa_raw3")
+        goal_blocks = []
+        for c in range(CHUNKS):
+            block = sb([P, P], F32, "goal_block%d" % c)
+            nc.sync.dma_start(out=block[:], in_=goal[c * P : (c + 1) * P, c * P : (c + 1) * P])
+            goal_blocks.append(block)
         lam_sb = []
         for h in range(2):
             pair = sb([P, 2, N], F32, "lam%d" % h)
             nc.sync.dma_start(out=pair[:], in_=lam[h * HALF : (h + 1) * HALF, :].rearrange("(c p) n -> p c n", p=P))
             lam_sb.extend([pair[:, 0, :], pair[:, 1, :]])
+        load_scales(nc.gpsimd, x_bytes, x_scales, X_ROW)
+        wgt_col = load_factor(nc.gpsimd, wgt, "wgt_col")
+        nc.gpsimd.dma_start(out=mean_rows[0:CHUNKS, :], in_=mean[0:1, :].rearrange("o (c q) -> (o c) q", q=P))
 
-        wgt_col = sb([P, PACK], F32, "wgt_col")
-        nc.gpsimd.dma_start(out=wgt_col[:], in_=wgt.rearrange("(p j) o -> p (j o)", j=PACK))
-
-        def spread(col, name, tag=None):
+        def spread(col, name, after=None):
             bank = spread_pool.tile([P, PACK, P], F32, name="spread", tag="spread")
             for j in range(PACK):
                 nc.tensor.transpose(bank[:, j, :], col[:, j : j + 1].to_broadcast([P, P]), ident[:])
-            row = sb([P, P, PACK], F32, name, tag)
-            nc.scalar.activation(out=row[:], in_=bank[:].rearrange("q j p -> q p j"), func=ACT.Copy)
-            return row[:].rearrange("q p j -> q (p j)")
+            row = sb([P, 2, P, 2], F32, name, after)
+            nc.scalar.activation(out=row[:], in_=bank[:].rearrange("q (u e) p -> q u p e", e=2), func=ACT.Copy)
+            return row
 
-        inv_row = spread(inv_col, "inv_row")
-
-        def gather(window, dtype, offsets, name, tag=None):
-            picked = sb([P, S], dtype, name, tag)
+        def gather(window, dtype, offsets, name, after=None):
+            picked = sb([P, S], dtype, name, after)
             nc.vector.tensor_copy(picked[:], window[:].indirect(offsets[:]))
             return picked
 
         def quantize(grouped, codes, scales):
             nc.vector.quantize_mx(out=codes.bitcast(FP8X4), scales=scales, in_=grouped[:].rearrange("p c j -> p (c j)"))
 
-        def weight_chunk(halves, c, name):
-            raw = halves[c // 2][:, :, (c % 2) * P : (c % 2 + 1) * P]
-            grouped = sb([P, P, PACK], BF16, "%s_grouped%d" % (name, c))
-            nc.scalar.copy(
-                out=grouped[:].rearrange("p (c i) j -> p c j i", i=4),
-                in_=raw.rearrange("p j (c i) -> p c j i", i=4),
-            )
-            codes = sb([P, P], U32, "%s_codes%d" % (name, c))
-            scales = sb([P, P], U8, "%s_scales%d" % (name, c))
-            quantize(grouped, codes[:], scales[:])
-            return codes, scales
+        def weight_pair(raw, first, name, after):
+            codes = sb([P, HALF], U32, name + "_codes%d" % first, after)
+            scales = sb([P, HALF], U8, name + "_scales%d" % first)
+            pair = []
+            for c in range(2):
+                cols = slice(c * P, (c + 1) * P)
+                grouped = sb([P, P, PACK], BF16, name + "_grouped%d" % (first + c))
+                nc.scalar.copy(
+                    out=grouped[:].rearrange("p (c i) j -> p c j i", i=4),
+                    in_=raw[first + c].rearrange("p j (c i) -> p c j i", i=4),
+                )
+                quantize(grouped, codes[:, cols], scales[:, cols])
+                pair.append((codes[:, cols], scales[:, cols]))
+            return pair
 
-        def project(w_chunk, picked, row0):
-            bank = acc_pool.tile([P, S], F32, name="acc", tag="acc")
+        def product(lhs, rhs):
+            bank = acc_pool.tile([P, N], F32, name="acc", tag="acc")
             nc.tensor.matmul_mx(
                 out=bank[:],
-                lhsT=w_chunk[0][:].bitcast(FP8X4),
-                lhsT_scale=w_chunk[1][:],
-                rhs=picked[0][:].bitcast(FP8X4),
-                rhs_scale=picked[1][row0:P, :],
+                lhsT=lhs[0].bitcast(FP8X4),
+                lhsT_scale=lhs[1],
+                rhs=rhs[0].bitcast(FP8X4),
+                rhs_scale=rhs[1],
                 start=True,
                 stop=True,
             )
             return bank
 
-        def turn(chunks, name, tag=None):
-            bank = turn_pool.tile([P, len(chunks), 2, P], F32, name="turned", tag="turned")
-            for c, rounded in enumerate(chunks):
-                words = rounded[:].bitcast(F32)
+        def by_word(ap):
+            return ap.rearrange("q (p u e) -> q u p e", u=2, e=2)
+
+        def turn(rounded, name, after=None):
+            bank = turn_pool.tile([P, len(rounded), 2, P], F32, name="turned", tag="turned")
+            for c, values in enumerate(rounded):
+                words = values.bitcast(F32)
                 for u in range(2):
-                    nc.tensor.transpose(bank[:, c, u, :], words[:, u : S // 2 : 2], ident[:])
-            grouped = sb([P, len(chunks) * P, PACK], BF16, name, tag)
+                    nc.tensor.transpose(bank[:, c, u, :], words[:, u * P : (u + 1) * P], ident[:])
+            grouped = sb([P, len(rounded) * P, PACK], BF16, name, after)
             nc.scalar.copy(
                 out=grouped[:].bitcast(F32).rearrange("p (c r) u -> p c r u", r=P),
                 in_=bank[:].rearrange("p c u r -> p c r u"),
             )
             return grouped
 
-        e_scales_picked = gather(e_bytes, U8, par_sb, "e_scales_picked")
-        e_picked = (gather(e_table, U32, par_sb, "e_codes_picked"), e_scales_picked)
+        def scale_v_pair(banks, name, after):
+            rounded = sb([P, 2, S], BF16, name, after)
+            for c in range(2):
+                nc.vector.tensor_tensor(
+                    rounded[:, c, :].rearrange("q (u p e) -> q u p e", u=2, e=2), by_word(banks[c][:]), inv_row[:], ALU.mult
+                )
+            return [rounded[:, 0, :], rounded[:, 1, :]]
 
+        inv_row = spread(inv_col, "inv_row")
+        e_scales_picked = gather(e_bytes, U8, par_sb, "e_scales_picked")
+        wb_q = weight_pair(wb_raw, 0, "wb", "e_bytes")
+        e_picked = (gather(e_table, U32, par_sb, "e_codes_picked")[:], e_scales_picked[E_ROW:P, :])
+        x_scales_picked = gather(x_bytes, U8, offs_sb, "x_scales_picked")
+        wb_q = wb_q + weight_pair(wb_raw, 2, "wb", "x_bytes")
+        v_banks = [product(wb_q[c], e_picked) for c in range(CHUNKS)]
+        v_first = scale_v_pair(v_banks[:2], "v_rounded01", "wb_grouped2")
+        x_picked = (gather(x_table, U32, offs_sb, "x_codes_picked", "wb_grouped3")[:], x_scales_picked[X_ROW:P, :])
+        wa_q = weight_pair(wa_raw, 0, "wa", "x_table")
+        v_second = scale_v_pair(v_banks[2:], "v_rounded23", "wa_grouped0")
+        wa_q = wa_q + weight_pair(wa_raw, 2, "wa", "wa_grouped1")
+
+        wgt_row = spread(wgt_col, "wgt_row", "wa_raw01")
+        mean_bank = spread_pool.tile([P, P], F32, name="spread", tag="spread")
+        nc.tensor.transpose(mean_bank[:], mean_rows[:], ident[:])
+        mean_col = sb([P, CHUNKS], F32, "mean_col", "wa_raw2")
+        nc.scalar.copy(out=mean_col[:], in_=mean_bank[:, 0:CHUNKS])
+
+        def scale_a(c):
+            bank = product(wa_q[c], x_picked)
+            rounded = sb([P, S], BF16, "a_rounded%d" % c)
+            for u in range(2):
+                nc.vector.scalar_tensor_tensor(
+                    rounded[:, u * HALF : (u + 1) * HALF].rearrange("q (p e) -> q p e", e=2),
+                    by_word(bank[:])[:, u],
+                    mean_col[:, c : c + 1],
+                    wgt_row[:, u],
+                    ALU.subtract,
+                    ALU.mult,
+                )
+            return rounded[:]
+
+        a_rounded = [scale_a(c) for c in range(2)]
         v_codes = sb([P, N], U32, "v_codes")
         v_scales = sb([P, N], U8, "v_scales")
-        first = sb([P, HALF, PACK], BF16, "wb_first")
-        nc.scalar.copy(
-            out=first[:].rearrange("p (c i) j -> p c j i", i=4), in_=wb_raw[0][:].rearrange("p j (c i) -> p c j i", i=4)
-        )
-        first_codes = sb([P, HALF], U32, "wb_first_codes", "e_bytes")
-        first_scales = sb([P, HALF], U8, "wb_first_scales")
-        quantize(first, first_codes[:], first_scales[:])
-        wb_q = [(first_codes[:, c * P : (c + 1) * P], first_scales[:, c * P : (c + 1) * P]) for c in range(2)]
-        wb_q.extend(weight_chunk(wb_raw, c, "wb") for c in range(2, CHUNKS))
-        x_scales_picked = gather(x_bytes, U8, offs_sb, "x_scales_picked")
-        v_rounded = {}
-        v_banks = [project(wb_q[c], e_picked, E_ROW) for c in range(CHUNKS)]
+        for h, (pair, after) in enumerate(((v_first, "wa_raw3"), (v_second, None))):
+            cols = slice(h * HALF, (h + 1) * HALF)
+            quantize(turn(pair, "v_grouped%d" % h, after), v_codes[:, cols], v_scales[:, cols])
+        a_rounded.extend(scale_a(c) for c in range(2, CHUNKS))
 
-        v_first = sb([P, 2, S], BF16, "v_first", "wb_raw1")
+        a_q = []
+        for c in range(CHUNKS):
+            codes = sb([P, P], U32, "a_codes%d" % c)
+            scales = sb([P, P], U8, "a_scales%d" % c)
+            quantize(turn([a_rounded[c]], "a_grouped%d" % c), codes[:], scales[:])
+            a_q.append((codes[:], scales[:]))
 
-        def e_step(c):
-            rounded = v_first[:, c, :] if c < 2 else sb([P, S], BF16, "v_rounded%d" % c, {"2":"wa_grouped0","3":"wa_raw0"}.get(str(c)))
-            nc.vector.tensor_tensor(rounded[:], v_banks[c][:], inv_row, ALU.mult)
-            v_rounded[c] = rounded
-
-        x_picked = (gather(x_table, U32, offs_sb, "x_codes_picked"), x_scales_picked)
-        e_step(0)
-        e_step(1)
-
-        wgt_row = spread(wgt_col, "wgt_row", "wb_grouped3")
-
-        wa_q = {}
-        a_rounded = {}
-        a_q = {}
-        zs = {}
-        sq = {}
-
-        def w_step(c):
-            wa_q[c] = weight_chunk(wa_raw, c, "wa")
-
-        def a_step(c):
-            bank = project(wa_q[c], x_picked, X_ROW)
-            rounded = sb([P, S], BF16, "a_rounded%d" % c)
-            nc.vector.scalar_tensor_tensor(rounded[:], bank[:], mean_col[:, c : c + 1], wgt_row, ALU.subtract, ALU.mult)
-            a_rounded[c] = rounded
-
-        def v_step(c):
-            cols = slice(c * HALF, (c + 1) * HALF)
-            quantize(turn([v_rounded[2 * c], v_rounded[2 * c + 1]], "v_grouped%d" % c, {"0":"wa_grouped1"}.get(str(c))), v_codes[:, cols], v_scales[:, cols])
-
-        def t_step(c):
-            a_codes = sb([P, P], U32, "a_codes%d" % c)
-            a_scales = sb([P, P], U8, "a_scales%d" % c)
-            quantize(turn([a_rounded[c]], "a_grouped%d" % c), a_codes[:], a_scales[:])
-            a_q[c] = (a_codes, a_scales)
-
-        def z_step(c):
-            cols = slice(c * P, (c + 1) * P)
-            z = acc_pool.tile([P, N], F32, name="acc", tag="acc")
-            nc.tensor.matmul_mx(
-                out=z[:],
-                lhsT=a_q[c][0][:].bitcast(FP8X4),
-                lhsT_scale=a_q[c][1][:],
-                rhs=v_codes[:].bitcast(FP8X4),
-                rhs_scale=v_scales[:],
-                start=True,
-                stop=True,
-            )
+        squared = []
+        for c in range(CHUNKS):
+            diagonal = slice(c * P, (c + 1) * P)
+            z = product(a_q[c], (v_codes[:], v_scales[:]))
             missed = sb([P, P], F32, "missed%d" % c)
-            nc.vector.scalar_tensor_tensor(missed[:], ident[:], goal_col[:, c : c + 1], z[:, cols], ALU.mult, ALU.subtract)
-            squared = sb([P, N], F32, "squared%d" % c)
-            for lo, hi in ((0, c * P), ((c + 1) * P, N)):
+            nc.vector.tensor_tensor(missed[:], z[:, diagonal], goal_blocks[c][:], ALU.subtract)
+            square = sb([P, N], F32, "squared%d" % c)
+            outside = ((0, c * P), ((c + 1) * P, N)) if c < CHUNKS - 1 else ((0, HALF), (HALF, c * P))
+            for lo, hi in outside:
                 if hi > lo:
-                    nc.scalar.activation(out=squared[:, lo:hi], in_=z[:, lo:hi], func=ACT.Square)
-            nc.scalar.activation(out=squared[:, cols], in_=missed[:], func=ACT.Square)
-            sq[c] = squared
+                    nc.scalar.activation(out=square[:, lo:hi], in_=z[:, lo:hi], func=ACT.Square)
+            nc.scalar.activation(out=square[:, diagonal], in_=missed[:], func=ACT.Square)
+            squared.append(square)
 
-        def o_step(c):
-            cols = slice(c * P, (c + 1) * P)
+        for c in range(CHUNKS):
             result = sb([P, N], F32, "result%d" % c)
-            nc.vector.tensor_tensor(result[:], sq[c][:], lam_sb[c], ALU.mult)
-            nc.sync.dma_start(out=out[cols, :], in_=result[:])
-
-        w_step(0)
-        w_step(1)
-        e_step(2)
-        e_step(3)
-        w_step(2)
-        w_step(3)
-        v_step(0)
-        v_step(1)
-        a_step(0)
-        t_step(0)
-        a_step(1)
-        t_step(1)
-        a_step(2)
-        t_step(2)
-        a_step(3)
-        t_step(3)
-        z_step(0)
-        z_step(1)
-        z_step(2)
-        z_step(3)
-        o_step(0)
-        o_step(1)
-        o_step(2)
-        o_step(3)
+            for lo, hi in ((0, N),) if c < CHUNKS - 1 else ((0, HALF), (HALF, N)):
+                nc.vector.tensor_tensor(result[:, lo:hi], squared[c][:, lo:hi], lam_sb[c][:, lo:hi], ALU.mult)
+                nc.sync.dma_start(out=out[c * P : (c + 1) * P, lo:hi], in_=result[:, lo:hi])

@@ -5,6 +5,7 @@ from concourse.masks import make_identity
 
 K, T, S, N = 512, 2048, 512, 512
 FLOPS = 3 * 2 * K * S * N
+BYTES = 2 * (K * T + K // 32 * T) + 4 * 4 * N * N + 4 * (2 * N + 2 * S) + 2 * 128 * (S // 16) * 2
 
 F32 = mybir.dt.float32
 BF16 = mybir.dt.bfloat16
@@ -29,7 +30,7 @@ def tile_picked_ybarlow_loss_p_kernel(
     nc = tc.nc
     with ExitStack() as ctx:
         keep = ctx.enter_context(tc.tile_pool(name="keep", bufs=1))
-        acc_pool = ctx.enter_context(tc.psum_pool(name="acc", bufs=4))
+        acc_pool = ctx.enter_context(tc.psum_pool(name="acc", bufs=CHUNKS))
         turn_pool = ctx.enter_context(tc.psum_pool(name="turn", bufs=2))
         spread_pool = ctx.enter_context(tc.psum_pool(name="spread", bufs=2))
 
@@ -48,9 +49,9 @@ def tile_picked_ybarlow_loss_p_kernel(
         nc.vector.memset(x_bytes[:].bitcast(I32), 0)
         nc.vector.memset(mean_rows[:], 0.0)
 
-        def load_scales(queue, tile, scales, row0):
+        def load_scales(window, scales, row0):
             for r in range(4):
-                queue.dma_start(out=tile[row0 + r : P : 32, :].bitcast(I32), in_=scales[0, r:16:4, :].bitcast(I32))
+                nc.sync.dma_start(out=window[row0 + r : P : 32, :].bitcast(I32), in_=scales[0, r:16:4, :].bitcast(I32))
 
         def load_words(words, name):
             table = sb([P, T], U32, name)
@@ -70,9 +71,10 @@ def tile_picked_ybarlow_loss_p_kernel(
         nc.sync.dma_start(par_sb[:], par)
         inv_col = load_factor(nc.scalar, inv, "inv_col")
         wb_raw = load_columns(wb, 0, HALF, "wb_raw01")
-        load_scales(nc.sync, e_bytes, e_scales, E_ROW)
+        load_scales(e_bytes, e_scales, E_ROW)
         e_table = load_words(e_words, "e_table")
         nc.sync.dma_start(offs_sb[:], offs)
+        load_scales(x_bytes, x_scales, X_ROW)
         wb_raw = wb_raw + load_columns(wb, HALF, N, "wb_raw23")
         x_table = load_words(x_words, "x_table")
         wa_raw = load_columns(wa, 0, HALF, "wa_raw01")
@@ -82,12 +84,11 @@ def tile_picked_ybarlow_loss_p_kernel(
             block = sb([P, P], F32, "goal_block%d" % c)
             nc.sync.dma_start(out=block[:], in_=goal[c * P : (c + 1) * P, c * P : (c + 1) * P])
             goal_blocks.append(block)
-        lam_sb = []
+        lam_rows = []
         for h in range(2):
-            pair = sb([P, 2, N], F32, "lam%d" % h)
-            nc.sync.dma_start(out=pair[:], in_=lam[h * HALF : (h + 1) * HALF, :].rearrange("(c p) n -> p c n", p=P))
-            lam_sb.extend([pair[:, 0, :], pair[:, 1, :]])
-        load_scales(nc.gpsimd, x_bytes, x_scales, X_ROW)
+            lam_half = sb([P, 2, N], F32, "lam%d" % h)
+            nc.sync.dma_start(out=lam_half[:], in_=lam[h * HALF : (h + 1) * HALF, :].rearrange("(c p) n -> p c n", p=P))
+            lam_rows.extend([lam_half[:, 0, :], lam_half[:, 1, :]])
         wgt_col = load_factor(nc.gpsimd, wgt, "wgt_col")
         nc.gpsimd.dma_start(out=mean_rows[0:CHUNKS, :], in_=mean[0:1, :].rearrange("o (c q) -> (o c) q", q=P))
 
@@ -99,18 +100,18 @@ def tile_picked_ybarlow_loss_p_kernel(
             nc.scalar.activation(out=row[:], in_=bank[:].rearrange("q (u e) p -> q u p e", e=2), func=ACT.Copy)
             return row
 
-        def gather(window, dtype, offsets, name, after=None):
-            picked = sb([P, S], dtype, name, after)
+        def gather(window, dtype, offsets, name):
+            picked = sb([P, S], dtype, name)
             nc.vector.tensor_copy(picked[:], window[:].indirect(offsets[:]))
             return picked
 
         def quantize(grouped, codes, scales):
             nc.vector.quantize_mx(out=codes.bitcast(FP8X4), scales=scales, in_=grouped[:].rearrange("p c j -> p (c j)"))
 
-        def weight_pair(raw, first, name, after):
+        def weight_pair(raw, first, name, after=None):
             codes = sb([P, HALF], U32, name + "_codes%d" % first, after)
             scales = sb([P, HALF], U8, name + "_scales%d" % first)
-            pair = []
+            operands = []
             for c in range(2):
                 cols = slice(c * P, (c + 1) * P)
                 grouped = sb([P, P, PACK], BF16, name + "_grouped%d" % (first + c))
@@ -119,8 +120,8 @@ def tile_picked_ybarlow_loss_p_kernel(
                     in_=raw[first + c].rearrange("p j (c i) -> p c j i", i=4),
                 )
                 quantize(grouped, codes[:, cols], scales[:, cols])
-                pair.append((codes[:, cols], scales[:, cols]))
-            return pair
+                operands.append((codes[:, cols], scales[:, cols]))
+            return operands
 
         def product(lhs, rhs):
             bank = acc_pool.tile([P, N], F32, name="acc", tag="acc")
@@ -135,15 +136,15 @@ def tile_picked_ybarlow_loss_p_kernel(
             )
             return bank
 
-        def by_word(ap):
+        def by_pair(ap):
             return ap.rearrange("q (p u e) -> q u p e", u=2, e=2)
 
         def turn(rounded, name, after=None):
             bank = turn_pool.tile([P, len(rounded), 2, P], F32, name="turned", tag="turned")
             for c, values in enumerate(rounded):
-                words = values.bitcast(F32)
+                pairs = values.bitcast(F32)
                 for u in range(2):
-                    nc.tensor.transpose(bank[:, c, u, :], words[:, u * P : (u + 1) * P], ident[:])
+                    nc.tensor.transpose(bank[:, c, u, :], pairs[:, u * P : (u + 1) * P], ident[:])
             grouped = sb([P, len(rounded) * P, PACK], BF16, name, after)
             nc.scalar.copy(
                 out=grouped[:].bitcast(F32).rearrange("p (c r) u -> p c r u", r=P),
@@ -155,27 +156,27 @@ def tile_picked_ybarlow_loss_p_kernel(
             rounded = sb([P, 2, S], BF16, name, after)
             for c in range(2):
                 nc.vector.tensor_tensor(
-                    rounded[:, c, :].rearrange("q (u p e) -> q u p e", u=2, e=2), by_word(banks[c][:]), inv_row[:], ALU.mult
+                    rounded[:, c, :].rearrange("q (u p e) -> q u p e", u=2, e=2), by_pair(banks[c][:]), inv_row[:], ALU.mult
                 )
             return [rounded[:, 0, :], rounded[:, 1, :]]
 
         inv_row = spread(inv_col, "inv_row")
         e_scales_picked = gather(e_bytes, U8, par_sb, "e_scales_picked")
-        wb_q = weight_pair(wb_raw, 0, "wb", "e_bytes")
+        wb_q = weight_pair(wb_raw, 0, "wb", after="e_bytes")
         e_picked = (gather(e_table, U32, par_sb, "e_codes_picked")[:], e_scales_picked[E_ROW:P, :])
         x_scales_picked = gather(x_bytes, U8, offs_sb, "x_scales_picked")
-        wb_q = wb_q + weight_pair(wb_raw, 2, "wb", "x_bytes")
+        wb_q = wb_q + weight_pair(wb_raw, 2, "wb")
         v_banks = [product(wb_q[c], e_picked) for c in range(CHUNKS)]
-        v_first = scale_v_pair(v_banks[:2], "v_rounded01", "wb_grouped2")
-        x_picked = (gather(x_table, U32, offs_sb, "x_codes_picked", "wb_grouped3")[:], x_scales_picked[X_ROW:P, :])
-        wa_q = weight_pair(wa_raw, 0, "wa", "x_table")
-        v_second = scale_v_pair(v_banks[2:], "v_rounded23", "wa_grouped0")
-        wa_q = wa_q + weight_pair(wa_raw, 2, "wa", "wa_grouped1")
+        v_first = scale_v_pair(v_banks[:2], "v_rounded01", after="wb_raw23")
+        x_picked = (gather(x_table, U32, offs_sb, "x_codes_picked")[:], x_scales_picked[X_ROW:P, :])
+        wa_q = weight_pair(wa_raw, 0, "wa")
+        v_second = scale_v_pair(v_banks[2:], "v_rounded23", after="wa_raw01")
+        wa_q = wa_q + weight_pair(wa_raw, 2, "wa")
 
-        wgt_row = spread(wgt_col, "wgt_row", "wa_raw01")
+        wgt_row = spread(wgt_col, "wgt_row", after="wb_grouped3")
         mean_bank = spread_pool.tile([P, P], F32, name="spread", tag="spread")
         nc.tensor.transpose(mean_bank[:], mean_rows[:], ident[:])
-        mean_col = sb([P, CHUNKS], F32, "mean_col", "wa_raw2")
+        mean_col = sb([P, CHUNKS], F32, "mean_col", after="wb_grouped2")
         nc.scalar.copy(out=mean_col[:], in_=mean_bank[:, 0:CHUNKS])
 
         def scale_a(c):
@@ -184,7 +185,7 @@ def tile_picked_ybarlow_loss_p_kernel(
             for u in range(2):
                 nc.vector.scalar_tensor_tensor(
                     rounded[:, u * HALF : (u + 1) * HALF].rearrange("q (p e) -> q p e", e=2),
-                    by_word(bank[:])[:, u],
+                    by_pair(bank[:])[:, u],
                     mean_col[:, c : c + 1],
                     wgt_row[:, u],
                     ALU.subtract,
@@ -195,9 +196,9 @@ def tile_picked_ybarlow_loss_p_kernel(
         a_rounded = [scale_a(c) for c in range(2)]
         v_codes = sb([P, N], U32, "v_codes")
         v_scales = sb([P, N], U8, "v_scales")
-        for h, (pair, after) in enumerate(((v_first, "wa_raw3"), (v_second, None))):
+        for h, (v_half, after) in enumerate(((v_first, "wa_raw3"), (v_second, None))):
             cols = slice(h * HALF, (h + 1) * HALF)
-            quantize(turn(pair, "v_grouped%d" % h, after), v_codes[:, cols], v_scales[:, cols])
+            quantize(turn(v_half, "v_grouped%d" % h, after), v_codes[:, cols], v_scales[:, cols])
         a_rounded.extend(scale_a(c) for c in range(2, CHUNKS))
 
         a_q = []
@@ -224,5 +225,5 @@ def tile_picked_ybarlow_loss_p_kernel(
         for c in range(CHUNKS):
             result = sb([P, N], F32, "result%d" % c)
             for lo, hi in ((0, N),) if c < CHUNKS - 1 else ((0, HALF), (HALF, N)):
-                nc.vector.tensor_tensor(result[:, lo:hi], squared[c][:, lo:hi], lam_sb[c][:, lo:hi], ALU.mult)
+                nc.vector.tensor_tensor(result[:, lo:hi], squared[c][:, lo:hi], lam_rows[c][:, lo:hi], ALU.mult)
                 nc.sync.dma_start(out=out[c * P : (c + 1) * P, lo:hi], in_=result[:, lo:hi])

from contextlib import ExitStack

import concourse.mybir as mybir
from concourse.masks import make_identity

K, T, S, N = 512, 2048, 512, 512
FLOPS = 3 * 2 * K * S * N
BYTES = 2 * (K * T + K // 32 * T) + 4 * 4 * N * N + 4 * (2 * N + 2 * S) + 2 * 128 * (S // 16) * 2

F32 = mybir.dt.float32
BF16 = mybir.dt.bfloat16
I32 = mybir.dt.int32
U32 = mybir.dt.uint32
U16 = mybir.dt.uint16
U8 = mybir.dt.uint8
FP8X4 = mybir.dt.float8_e4m3fn_x4
ALU = mybir.AluOpType
ACT = mybir.ActivationFunctionType

P = 128
PACK = 4
CHUNKS = N // P
HALF = N // 2
E_ROW, X_ROW = 0, 4


def tile_picked_ybarlow_loss_p_kernel(
    tc, x_words, x_scales, e_words, e_scales, wa, mean, wgt, wb, inv, goal, lam, offs, par, out
):
    nc = tc.nc
    with ExitStack() as ctx:
        keep = ctx.enter_context(tc.tile_pool(name="keep", bufs=1))
        acc_pool = ctx.enter_context(tc.psum_pool(name="acc", bufs=CHUNKS))
        turn_pool = ctx.enter_context(tc.psum_pool(name="turn", bufs=2))
        spread_pool = ctx.enter_context(tc.psum_pool(name="spread", bufs=2))

        def sb(shape, dtype, name, after=None):
            return keep.tile(shape, dtype, name=name, tag=after or name, align_bytes=64)

        par_sb = keep.tile([P, S // 16], U16, name="par_sb")
        offs_sb = keep.tile([P, S // 16], U16, name="offs_sb")
        e_bytes = sb([P, T], U8, "e_bytes")
        x_bytes = sb([P, T], U8, "x_bytes")
        ident = sb([P, P], F32, "ident")
        mean_rows = sb([P, P], F32, "mean_rows")
        nc.gpsimd.memset(ident[:], 0.0)
        nc.gpsimd.memset(e_bytes[:].bitcast(I32), 0)
        make_identity(nc, ident[:], nomemset=True)
        nc.vector.memset(x_bytes[:].bitcast(I32), 0)
        nc.vector.memset(mean_rows[:], 0.0)

        def load_scales(window, scales, row0):
            for r in range(4):
                nc.sync.dma_start(out=window[row0 + r : P : 32, :].bitcast(I32), in_=scales[0, r:16:4, :].bitcast(I32))

        def load_words(words, name):
            table = sb([P, T], U32, name)
            nc.sync.dma_start(out=table[:].bitcast(I32), in_=words[0].rearrange("p n t -> p (n t)").bitcast(I32))
            return table

        def load_columns(w, lo, hi, name):
            raw = sb([P, PACK, hi - lo], F32, name)
            nc.sync.dma_start(out=raw[:], in_=w.rearrange("(p j) c -> p j c", j=PACK)[:, :, lo:hi])
            return [raw[:, :, c : c + P] for c in range(0, hi - lo, P)]

        def load_factor(queue, factor, name):
            col = sb([P, PACK], F32, name)
            queue.dma_start(out=col[:], in_=factor.rearrange("(p j) o -> p (j o)", j=PACK))
            return col

        nc.sync.dma_start(par_sb[:], par)
        inv_col = load_factor(nc.scalar, inv, "inv_col")
        wb_raw = load_columns(wb, 0, HALF, "wb_raw01")
        load_scales(e_bytes, e_scales, E_ROW)
        e_table = load_words(e_words, "e_table")
        nc.sync.dma_start(offs_sb[:], offs)
        load_scales(x_bytes, x_scales, X_ROW)
        wb_raw = wb_raw + load_columns(wb, HALF, N, "wb_raw23")
        x_table = load_words(x_words, "x_table")
        wa_raw = load_columns(wa, 0, HALF, "wa_raw01")
        wa_raw = wa_raw + load_columns(wa, 2 * P, 3 * P, "wa_raw2") + load_columns(wa, 3 * P, N, "wa_raw3")
        goal_blocks = []
        for c in range(CHUNKS):
            block = sb([P, P], F32, "goal_block%d" % c)
            nc.sync.dma_start(out=block[:], in_=goal[c * P : (c + 1) * P, c * P : (c + 1) * P])
            goal_blocks.append(block)
        lam_rows = []
        for h in range(2):
            lam_half = sb([P, 2, N], F32, "lam%d" % h)
            nc.sync.dma_start(out=lam_half[:], in_=lam[h * HALF : (h + 1) * HALF, :].rearrange("(c p) n -> p c n", p=P))
            lam_rows.extend([lam_half[:, 0, :], lam_half[:, 1, :]])
        wgt_col = load_factor(nc.gpsimd, wgt, "wgt_col")
        nc.gpsimd.dma_start(out=mean_rows[0:CHUNKS, :], in_=mean[0:1, :].rearrange("o (c q) -> (o c) q", q=P))

        def spread(col, name, after=None):
            bank = spread_pool.tile([P, PACK, P], F32, name="spread", tag="spread")
            for j in range(PACK):
                nc.tensor.transpose(bank[:, j, :], col[:, j : j + 1].to_broadcast([P, P]), ident[:])
            row = sb([P, 2, P, 2], F32, name, after)
            nc.scalar.activation(out=row[:], in_=bank[:].rearrange("q (u e) p -> q u p e", e=2), func=ACT.Copy)
            return row

        def gather(window, dtype, offsets, name):
            picked = sb([P, S], dtype, name)
            nc.vector.tensor_copy(picked[:], window[:].indirect(offsets[:]))
            return picked

        def quantize(grouped, codes, scales):
            nc.vector.quantize_mx(out=codes.bitcast(FP8X4), scales=scales, in_=grouped[:].rearrange("p c j -> p (c j)"))

        def weight_pair(raw, first, name, after=None):
            codes = sb([P, HALF], U32, name + "_codes%d" % first, after)
            scales = sb([P, HALF], U8, name + "_scales%d" % first)
            operands = []
            for c in range(2):
                cols = slice(c * P, (c + 1) * P)
                grouped = sb([P, P, PACK], BF16, name + "_grouped%d" % (first + c))
                nc.scalar.copy(
                    out=grouped[:].rearrange("p (c i) j -> p c j i", i=4),
                    in_=raw[first + c].rearrange("p j (c i) -> p c j i", i=4),
                )
                quantize(grouped, codes[:, cols], scales[:, cols])
                operands.append((codes[:, cols], scales[:, cols]))
            return operands

        def product(lhs, rhs):
            bank = acc_pool.tile([P, N], F32, name="acc", tag="acc")
            nc.tensor.matmul_mx(
                out=bank[:],
                lhsT=lhs[0].bitcast(FP8X4),
                lhsT_scale=lhs[1],
                rhs=rhs[0].bitcast(FP8X4),
                rhs_scale=rhs[1],
                start=True,
                stop=True,
            )
            return bank

        def by_pair(ap):
            return ap.rearrange("q (p u e) -> q u p e", u=2, e=2)

        def turn(rounded, name, after=None):
            bank = turn_pool.tile([P, len(rounded), 2, P], F32, name="turned", tag="turned")
            for c, values in enumerate(rounded):
                pairs = values.bitcast(F32)
                for u in range(2):
                    nc.tensor.transpose(bank[:, c, u, :], pairs[:, u * P : (u + 1) * P], ident[:])
            grouped = sb([P, len(rounded) * P, PACK], BF16, name, after)
            nc.scalar.copy(
                out=grouped[:].bitcast(F32).rearrange("p (c r) u -> p c r u", r=P),
                in_=bank[:].rearrange("p c u r -> p c r u"),
            )
            return grouped

        def scale_v_pair(banks, name, after):
            rounded = sb([P, 2, S], BF16, name, after)
            for c in range(2):
                nc.vector.tensor_tensor(
                    rounded[:, c, :].rearrange("q (u p e) -> q u p e", u=2, e=2), by_pair(banks[c][:]), inv_row[:], ALU.mult
                )
            return [rounded[:, 0, :], rounded[:, 1, :]]

        inv_row = spread(inv_col, "inv_row")
        e_scales_picked = gather(e_bytes, U8, par_sb, "e_scales_picked")
        wb_q = weight_pair(wb_raw, 0, "wb", after="e_bytes")
        e_picked = (gather(e_table, U32, par_sb, "e_codes_picked")[:], e_scales_picked[E_ROW:P, :])
        x_scales_picked = gather(x_bytes, U8, offs_sb, "x_scales_picked")
        wb_q = wb_q + weight_pair(wb_raw, 2, "wb")
        v_banks = [product(wb_q[c], e_picked) for c in range(CHUNKS)]
        v_first = scale_v_pair(v_banks[:2], "v_rounded01", after="wb_raw23")
        x_picked = (gather(x_table, U32, offs_sb, "x_codes_picked")[:], x_scales_picked[X_ROW:P, :])
        wa_q = weight_pair(wa_raw, 0, "wa")
        v_second = scale_v_pair(v_banks[2:], "v_rounded23", after="wa_raw01")
        wa_q = wa_q + weight_pair(wa_raw, 2, "wa")

        wgt_row = spread(wgt_col, "wgt_row", after="wb_grouped3")
        mean_bank = spread_pool.tile([P, P], F32, name="spread", tag="spread")
        nc.tensor.transpose(mean_bank[:], mean_rows[:], ident[:])
        mean_col = sb([P, CHUNKS], F32, "mean_col", after="wb_grouped2")
        nc.scalar.copy(out=mean_col[:], in_=mean_bank[:, 0:CHUNKS])

        def scale_a(c):
            bank = product(wa_q[c], x_picked)
            rounded = sb([P, S], BF16, "a_rounded%d" % c)
            for u in range(2):
                nc.vector.scalar_tensor_tensor(
                    rounded[:, u * HALF : (u + 1) * HALF].rearrange("q (p e) -> q p e", e=2),
                    by_pair(bank[:])[:, u],
                    mean_col[:, c : c + 1],
                    wgt_row[:, u],
                    ALU.subtract,
                    ALU.mult,
                )
            return rounded[:]

        a_rounded = [scale_a(c) for c in range(2)]
        v_codes = sb([P, N], U32, "v_codes")
        v_scales = sb([P, N], U8, "v_scales")
        for h, (v_half, after) in enumerate(((v_first, "wa_raw3"), (v_second, None))):
            cols = slice(h * HALF, (h + 1) * HALF)
            quantize(turn(v_half, "v_grouped%d" % h, after), v_codes[:, cols], v_scales[:, cols])
        a_rounded.extend(scale_a(c) for c in range(2, CHUNKS))

        a_q = []
        for c in range(CHUNKS):
            codes = sb([P, P], U32, "a_codes%d" % c)
            scales = sb([P, P], U8, "a_scales%d" % c)
            quantize(turn([a_rounded[c]], "a_grouped%d" % c), codes[:], scales[:])
            a_q.append((codes[:], scales[:]))

        squared = []
        for c in range(CHUNKS):
            diagonal = slice(c * P, (c + 1) * P)
            z = product(a_q[c], (v_codes[:], v_scales[:]))
            missed = sb([P, P], F32, "missed%d" % c)
            nc.vector.tensor_tensor(missed[:], z[:, diagonal], goal_blocks[c][:], ALU.subtract)
            square = sb([P, N], F32, "squared%d" % c)
            outside = ((0, c * P), ((c + 1) * P, N)) if c < CHUNKS - 1 else ((0, HALF), (HALF, c * P))
            for lo, hi in outside:
                if hi > lo:
                    nc.scalar.activation(out=square[:, lo:hi], in_=z[:, lo:hi], func=ACT.Square)
            nc.scalar.activation(out=square[:, diagonal], in_=missed[:], func=ACT.Square)
            squared.append(square)

        for c in range(CHUNKS):
            result = sb([P, N], F32, "result%d" % c)
            for lo, hi in ((0, N),) if c < CHUNKS - 1 else ((0, HALF), (HALF, N)):
                nc.vector.tensor_tensor(result[:, lo:hi], squared[c][:, lo:hi], lam_rows[c][:, lo:hi], ALU.mult)
                nc.sync.dma_start(out=out[c * P : (c + 1) * P, lo:hi], in_=result[:, lo:hi])
